import numpy as np
import ml_dtypes


def mxq(x, axis, fmt="e4m3"):
    dtype, down = {"e4m3": (ml_dtypes.float8_e4m3fn, 7), "e5m2": (ml_dtypes.float8_e5m2, 14)}[fmt]
    v = np.moveaxis(np.asarray(x, np.float32).astype(ml_dtypes.bfloat16).astype(np.float64), axis, -1)
    blocks = v.reshape(v.shape[:-1] + (-1, 32))
    amax = np.abs(blocks).max(-1, keepdims=True)
    byte = np.maximum(np.where(amax > 0, np.frexp(amax)[1] - 1 + 127, 0) - down, 1)
    scale = np.exp2(byte - 127.0)
    codes = (blocks / scale).astype(np.float32).astype(dtype).astype(np.float64)
    return np.moveaxis((codes * scale).reshape(v.shape), -1, axis)


WIDE = False


def mx_kscale(k):
    if not WIDE:
        return np.ones(k)
    levels = np.array([10, -10, 5, -5, 0])
    if k % 512:
        return np.exp2(np.random.permutation(np.resize(levels, k // 32))).repeat(32)
    a = np.empty((k // 512, 16))
    for p in range(k // 512):
        a[p, :8] = np.random.permutation(np.resize(levels, 8))
        for g in range(8):
            far = levels[np.abs(levels - a[p, g]) >= 10]
            a[p, g + 8] = far[np.random.randint(len(far))]
    return np.exp2(a.ravel()).repeat(32)


def f64(x):
    return np.asarray(x).astype(np.float64)


def striped(idx):
    return np.tile(idx.reshape(-1, 16).T, (8, 1)).astype(np.uint16)


def unstriped(offs):
    return offs[:16].T.reshape(-1).astype(np.int64)


def striped8(idx):
    return np.concatenate([x.reshape(-1, 16).T for x in idx]).astype(np.uint16)


def runs(offs, k):
    lists = np.stack([offs[16 * r : 16 * r + 16].T.reshape(-1) for r in range(8)]).astype(np.int64)
    return lists[np.arange(k) % 512 // 64]


def pack_weight(w):
    k, n = w.shape
    w = f64(np.asarray(w, np.float32).astype(ml_dtypes.bfloat16)).reshape(k // 32, 32, n)
    amax = np.abs(w).max(1)
    byte = np.clip(np.where(amax > 0, np.frexp(amax)[1] - 1 + 127 - 7, 1), 1, 254)
    scaled = (w * np.exp2(127.0 - byte)[:, None, :]).reshape(k, n).astype(np.float32)
    words = np.ascontiguousarray(scaled.reshape(k // 512, 128, 4, n).transpose(0, 1, 3, 2)).astype(ml_dtypes.float8_e4m3fn).view(np.uint8)
    return words, np.ascontiguousarray(byte.astype(np.uint8).reshape(k // 512, 16, n))


def unpack_weight(words, scales):
    g, p, n, _ = words.shape
    vals = np.ascontiguousarray(words).view(ml_dtypes.float8_e4m3fn).astype(np.float64) * np.repeat(np.exp2(scales.astype(np.float64) - 127.0), 8, axis=1)[..., None]
    return vals.transpose(0, 1, 3, 2).reshape(g * 512, n)


E2M1 = np.array([0.0, 0.5, 1.0, 1.5, 2.0, 3.0, 4.0, 6.0, -0.0, -0.5, -1.0, -1.5, -2.0, -3.0, -4.0, -6.0])


def pack_fp4(w):
    k, n = w.shape
    w = f64(np.asarray(w, np.float32).astype(ml_dtypes.bfloat16)).reshape(k // 32, 32, n)
    amax = np.abs(w).max(1)
    mant, ex = np.frexp(amax / 6.0)
    byte = np.clip(np.where(amax > 0, np.where(mant > 0.5, ex, ex - 1) + 127, 1), 1, 254)
    scaled = (w * np.exp2(127.0 - byte)[:, None, :]).reshape(k, n).astype(np.float32)
    c = np.ascontiguousarray(scaled.reshape(k // 512, 128, 4, n).transpose(0, 1, 3, 2)).astype(ml_dtypes.float4_e2m1fn).view(np.uint8) & 0xF
    words = (c[..., 0::2] | (c[..., 1::2] << 4)).reshape(k // 512, 128, 2 * n)
    return np.ascontiguousarray(words), np.ascontiguousarray(byte.astype(np.uint8).reshape(k // 512, 16, n))


def unpack_fp4(words, scales):
    g, _, n = scales.shape
    words = np.ascontiguousarray(words).reshape(g, 128, n, 2)
    nib = np.empty((g, 128, n, 4), np.uint8)
    nib[..., 0::2] = words & 0xF
    nib[..., 1::2] = words >> 4
    vals = E2M1[nib] * np.repeat(np.exp2(scales.astype(np.float64) - 127.0), 8, axis=1)[..., None]
    return vals.transpose(0, 1, 3, 2).reshape(g * 512, n)


def planes(y):
    n, m = y.shape
    v = y.astype(np.float32).astype(ml_dtypes.bfloat16).astype(np.float64).reshape(n // 32, 32, m)
    top = np.abs(v).max(1)
    byte = np.clip(np.where(top > 0, np.frexp(top)[1] - 1 + 127 - 7, 1), 1, 254)
    codes = (v * np.exp2(127.0 - byte)[:, None, :]).reshape(n, m).astype(np.float32).astype(ml_dtypes.float8_e4m3fn).view(np.uint8)
    words = codes.reshape(n // 512, 128, 4, m).transpose(0, 1, 3, 2)
    return np.ascontiguousarray(words), np.ascontiguousarray(byte.astype(np.uint8).reshape(n // 512, 16, m))


K, T, S, V, N, H = 512, 2048, 512, 256, 512, 512


def setup_inputs():
    n = np.random.standard_normal
    s = mx_kscale(K)[:, None]
    u = mx_kscale(H)
    packed_xT = pack_weight(n((K, T)) * s)
    packed_w3 = pack_fp4(n((H, N)) / np.sqrt(H) / u[:, None])
    perm = np.stack([np.random.permutation(S) for _ in range(8)])
    return {
        "x_words": packed_xT[0],
        "x_scales": packed_xT[1],
        "w1": (n((K, H)) / np.sqrt(K) / s * u).astype(np.float32),
        "w2": (n((H, H)) / np.sqrt(H) / u[:, None] * u).astype(np.float32),
        "res": (2 * n((N, S))).astype(np.float32),
        "w3_words": packed_w3[0],
        "w3_scales": packed_w3[1],
        "offs": striped(np.random.permutation(T)[:S]),
        "la": striped8(perm[:, :V]),
        "lb": striped8(perm[:, V:]),
        "mate": striped8(np.stack([np.random.permutation(S) for _ in range(8)])),
    }


def reference(x_words, x_scales, w1, w2, res, w3_words, w3_scales, offs, la, lb, mate):
    xq = unpack_weight(x_words, x_scales)[:, unstriped(offs)]
    y = mxq(f64(w1), 0, "e4m3").T @ xq
    a = y[np.arange(H)[:, None], runs(la, H)]
    b = y[np.arange(H)[:, None], runs(lb, H)]
    df = a - b
    sm = a + b
    p = np.zeros((H, S))
    p[np.arange(H)[:, None], runs(la, H)] = sm
    z = p.copy()
    z[np.arange(H)[:, None], runs(lb, H)] = df
    h = mxq(f64(w2), 0, "e4m3").T @ mxq(z, 0, "e4m3")
    z2 = h - (h[np.arange(H)[:, None], runs(mate, H)])
    out_0 = f64(res) + 0.5 * ((unpack_fp4(w3_words, w3_scales).T @ mxq(z2, 0, "e4m3")))
    return (out_0,) + planes(out_0)

@@ -1,0 +1,218 @@
+from contextlib import ExitStack
+
+import concourse.mybir as mybir
+
+K, T, S, V, N, H = 512, 2048, 512, 256, 512, 512
+FLOPS = 2 * K * H * S + 2 * H * H * S + 2 * H * N * S
+
+F32 = mybir.dt.float32
+BF16 = mybir.dt.bfloat16
+I32 = mybir.dt.int32
+U32 = mybir.dt.uint32
+U16 = mybir.dt.uint16
+U8 = mybir.dt.uint8
+FP8X4 = mybir.dt.float8_e4m3fn_x4
+FP4X4 = mybir.dt.float4_e2m1fn_x4
+ADD = mybir.AluOpType.add
+MULT = mybir.AluOpType.mult
+COPY = mybir.ActivationFunctionType.Copy
+
+P = 128
+R = 4
+CH = 128
+NCH = S // CH
+PIECES = [slice(0, 256), slice(256, 384), slice(384, 512)]
+HALVES = [slice(0, 256), slice(256, 512)]
+WHOLE = [slice(0, 512)]
+
+
+def tile_picked_crossfft_none_po_kernel(
+    tc, x_words, x_scales, w1, w2, res, w3_words, w3_scales, offs, la, lb, mate, out_0, out_1, out_2
+):
+    nc = tc.nc
+    with ExitStack() as ctx:
+        sb = ctx.enter_context(tc.tile_pool(name="sb", bufs=1))
+        ps = ctx.enter_context(tc.psum_pool(name="ps", bufs=1))
+
+        def tile(name, shape, dtype, slot=None):
+            return sb.tile(shape, dtype, name=name, tag=slot or name, align_bytes=64)
+
+        def load_scale_rows(eng, dst, src):
+            for q in range(4):
+                eng.dma_start(out=dst[32 * q : 32 * q + 4, :].bitcast(I32), in_=src[0, 4 * q : 4 * q + 4, :].bitcast(I32))
+
+        offs_t = tile("offs_t", [P, S // 16], U16)
+        la_t = tile("la_t", [P, V // 16], U16)
+        lb_t = tile("lb_t", [P, V // 16], U16)
+        mate_t = tile("mate_t", [P, S // 16], U16)
+        xs = tile("xs", [P, T], U8)
+        xw = tile("xw", [P, T], I32)
+        w1_raw = [tile(f"w1_raw{u}", [P, R, H // 2], F32) for u in range(2)]
+
+        nc.vector.memset(xs[:].bitcast(I32), 0)
+        nc.sync.dma_start(offs_t[:], offs)
+        w3w = tile("w3w", [P, 2 * N], U8)
+        nc.sync.dma_start(out=w3w[:].bitcast(I32), in_=w3_words[0].bitcast(I32))
+        nc.sync.dma_start(la_t[:], la)
+        nc.sync.dma_start(out=xw[:], in_=x_words[0].rearrange("p n r -> p (n r)").bitcast(I32))
+        nc.sync.dma_start(lb_t[:], lb)
+        load_scale_rows(nc.sync, xs, x_scales)
+        w1_rows = w1.rearrange("(p j) c -> p j c", j=R)
+        for u in range(2):
+            nc.sync.dma_start(out=w1_raw[u][:], in_=w1_rows[:, :, u * (H // 2) : (u + 1) * (H // 2)])
+        nc.sync.dma_start(mate_t[:], mate)
+        w3w_d = tile("w3w_d", [P, 2 * N], U8)
+        nc.vector.tensor_copy(w3w_d[:].rearrange("p (t m e) -> p m t e", t=R, e=2), w3w[:].rearrange("p (m t e) -> p m t e", t=R, e=2))
+
+        xg_s = tile("xg_s", [P, S], U8)
+        xg_w = tile("xg_w", [P, S], U32)
+        nc.vector.tensor_copy(xg_w[:], xw[:].bitcast(U32).indirect(offs_t[:]))
+        nc.vector.tensor_copy(xg_s[:], xs[:].indirect(offs_t[:]))
+
+        w1_b = tile("w1_b", [P, R * H], BF16)
+        w1_v = w1_b[:].rearrange("p (t m j) -> p m t j", t=R, j=R)
+        nc.scalar.activation(w1_v[:, 0:64], w1_raw[0][:].rearrange("p j (m t) -> p m t j", t=R), COPY)
+        w1_c = tile("w1_c", [P, H], U32)
+        w1_s = tile("w1_s", [P, H], U8)
+        w1_hi = w1_raw[1][:].rearrange("p j (m t) -> p m t j", t=R)
+        y = [tile(f"y{t}", [P, S], F32) for t in range(R)]
+        nc.scalar.copy(w1_v[:, 64:128, 2:4, :], w1_hi[:, :, 2:4, :])
+        for t in range(2):
+            nc.vector.tensor_copy(w1_v[:, 64:128, t, :], w1_hi[:, :, t, :])
+            cols = slice(t * P, (t + 1) * P)
+            nc.vector.quantize_mx(out=w1_c[:, cols].bitcast(FP8X4), scales=w1_s[:, cols], in_=w1_b[:, t * 512 : (t + 1) * 512])
+        nc.vector.quantize_mx(out=w1_c[:, 256:512].bitcast(FP8X4), scales=w1_s[:, 256:512], in_=w1_b[:, 1024:2048])
+
+        def product(name, tags, pieces, codes, scales, rhs, rhs_scale, leave):
+            for tag, cols in zip(tags, pieces):
+                acc = ps.tile([P, cols.stop - cols.start], F32, name=f"{name}_{tag}", tag=tag)
+                nc.tensor.matmul_mx(out=acc[:], lhsT=codes.bitcast(FP8X4), lhsT_scale=scales,
+                                    rhs=rhs[:, cols].bitcast(FP8X4), rhs_scale=rhs_scale[:, cols], start=True, stop=True)
+                leave(acc, cols)
+
+        for t in range(R):
+            cols = slice(t * P, (t + 1) * P)
+            product(f"acc_y{t}", ["b0", "a0"] if t == 0 else [f"a{t}"], HALVES if t == 0 else WHOLE, w1_c[:, cols], w1_s[:, cols], xg_w, xg_s,
+                    lambda acc, cs: nc.scalar.copy(y[t][:, cs], acc[:]))
+
+        w2_raw = [tile(f"w2_raw{u}", [P, R, H // 2], F32, slot=f"w1_raw{u}") for u in range(2)]
+        w2_rows = w2.rearrange("(p j) c -> p j c", j=R)
+        for u in range(2):
+            nc.sync.dma_start(out=w2_raw[u][:], in_=w2_rows[:, :, u * (H // 2) : (u + 1) * (H // 2)])
+        w3s = tile("w3s", [P, N], U8, slot="w1_b")
+        nc.vector.memset(w3s[:].bitcast(I32), 0)
+        load_scale_rows(nc.sync, w3s, w3_scales)
+        res_t = tile("res_t", [P, R, S], F32, slot="xw")
+        nc.sync.dma_start(out=res_t[:], in_=res.rearrange("(p t) c -> p t c", t=R))
+
+        a = [tile(f"a{t}", [P, V], F32) for t in range(R)]
+        b = [tile(f"b{t}", [P, V], F32) for t in range(R)]
+        nb = [tile(f"nb{t}", [P, V], F32) for t in range(R)]
+        z = [tile(f"z{t}", [P, S], F32) for t in range(R)]
+        z_b = tile("z_b", [P, S, R], BF16)
+        w2_b = tile("w2_b", [P, R * H], BF16)
+        w2_v = w2_b[:].rearrange("p (t m j) -> p m t j", t=R, j=R)
+        w2_in = [w2_raw[u][:].rearrange("p j (m t) -> p m t j", t=R) for u in range(2)]
+
+        def fetch_b(t):
+            nc.vector.tensor_copy(b[t][:], y[t][:].indirect(lb_t[:]))
+            nc.scalar.activation(nb[t][:], b[t][:], COPY, scale=-1.0)
+
+        def fetch_a(t):
+            nc.vector.tensor_copy(a[t][:], y[t][:].indirect(la_t[:]))
+
+        fetch_b(0)
+        fetch_a(0)
+        for t in range(R):
+            if t + 1 < R:
+                fetch_b(t + 1)
+            nc.vector.tensor_tensor(z[t][:].indirect(la_t[:]), a[t][:], b[t][:], ADD)
+            if t + 1 < R:
+                fetch_a(t + 1)
+            nc.vector.tensor_tensor(z[t][:].indirect(lb_t[:]), a[t][:], nb[t][:], ADD)
+            nc.scalar.copy(w2_v[:, 32 * t : 32 * t + 32], w2_in[t // 2][:, 32 * (t % 2) : 32 * (t % 2) + 32])
+            for cols in PIECES:
+                nc.scalar.copy(z_b[:, cols, t], z[t][:, cols])
+
+        w2_c = tile("w2_c", [P, H], U32, slot="a3")
+        w2_s = tile("w2_s", [P, H], U8)
+        nc.vector.quantize_mx(out=w2_c[:].bitcast(FP8X4), scales=w2_s[:], in_=w2_b[:])
+
+        z_c = tile("z_c", [P, S], U32)
+        z_s = tile("z_s", [P, S], U8)
+        for cols in PIECES:
+            nc.vector.quantize_mx(out=z_c[:, cols].bitcast(FP8X4), scales=z_s[:, cols],
+                                  in_=z_b[:, cols, :].rearrange("p c t -> p (c t)"))
+
+        w3s_d = tile("w3s_d", [P, N], U8, slot="z_b")
+        nc.vector.tensor_copy(w3s_d[:].rearrange("p (t m) -> p m t", t=R), w3s[:].rearrange("p (m t) -> p m t", t=R))
+        hneg = [tile(f"hneg{t}", [P, S], F32) for t in range(R)]
+        hpos = [tile(f"hpos{t}", [P, S], F32) for t in range(R)]
+        for t in range(R):
+            wc = slice(t * P, (t + 1) * P)
+
+            def leave(acc, cs):
+                nc.scalar.activation(hneg[t][:, cs], acc[:], COPY, scale=-1.0)
+                if t == 0:
+                    nc.vector.tensor_scalar(hpos[t][:, cs], hneg[t][:, cs], -1.0, None, MULT)
+                else:
+                    nc.scalar.copy(hpos[t][:, cs], acc[:])
+
+            product(f"acc_h{t}", ["b0", "a0", "a1"] if t == 0 else [f"b{t}"], PIECES if t == 0 else WHOLE, w2_c[:, wc], w2_s[:, wc], z_c, z_s, leave)
+
+        z2 = [tile(f"z2_{c}", [P, R, CH], F32) for c in range(NCH)]
+
+        def fetch_mate(t, c):
+            nc.vector.tensor_tensor(z2[c][:, t, :], hneg[t][:].indirect(mate_t[:, c * CH // 16 : (c + 1) * CH // 16]),
+                                    hpos[t][:, c * CH : (c + 1) * CH], ADD)
+
+        o_w = tile("o_w", [P, S], U32)
+        o_s = tile("o_s", [P, S], U8)
+        out_rows = out_0.rearrange("(p t) c -> p t c", t=R)
+        words = out_1[0].rearrange("p c r -> p (c r)").bitcast(I32)
+        z2_b = [tile(f"z2_b{c}", [P, CH, R], BF16) for c in range(NCH)]
+        z2_c = [tile(f"z2_c{c}", [P, CH], U32) for c in range(NCH)]
+        z2_s = [tile(f"z2_s{c}", [P, CH], U8) for c in range(NCH)]
+        o = [tile(f"o{c}", [P, R, CH], F32) for c in range(NCH)]
+        o_b = [tile(f"o_b{c}", [P, CH, R], BF16) for c in range(NCH)]
+        accs = {}
+
+        def interleave(c, dst, src):
+            if c == NCH - 1:
+                nc.vector.tensor_copy(dst[:], src[:].rearrange("p t c -> p c t"))
+            else:
+                nc.scalar.copy(dst[:], src[:].rearrange("p t c -> p c t"))
+
+        def stage_a(c):
+            for t in range(2, R):
+                fetch_mate(t, c)
+            interleave(c, z2_b[c], z2[c])
+
+        def stage_b(c):
+            nc.vector.quantize_mx(out=z2_c[c][:].bitcast(FP8X4), scales=z2_s[c][:], in_=z2_b[c][:].rearrange("p c t -> p (c t)"))
+            accs[c] = ps.tile([P, R, CH], F32, name=f"acc_o{c}", tag=f"a{c}")
+            for t in range(R):
+                nc.tensor.matmul_mx(out=accs[c][:, t, :], lhsT=w3w_d[:, 2 * t * P : 2 * (t + 1) * P].bitcast(FP4X4),
+                                    lhsT_scale=w3s_d[:, t * P : (t + 1) * P],
+                                    rhs=z2_c[c][:].bitcast(FP8X4), rhs_scale=z2_s[c][:], start=True, stop=True)
+
+        def stage_c(c):
+            nc.vector.scalar_tensor_tensor(o[c][:], accs[c][:], 0.5, res_t[:, :, c * CH : (c + 1) * CH], MULT, ADD)
+            nc.sync.dma_start(out=out_rows[:, :, c * CH : (c + 1) * CH], in_=o[c][:])
+            interleave(c, o_b[c], o[c])
+
+        def stage_d(c):
+            cols = slice(c * CH, (c + 1) * CH)
+            nc.vector.quantize_mx(out=o_w[:, cols].bitcast(FP8X4), scales=o_s[:, cols], in_=o_b[c][:].rearrange("p c t -> p (c t)"))
+            nc.sync.dma_start(out=words[:, cols], in_=o_w[:, cols].bitcast(I32))
+
+        for t in range(2):
+            for c in range(NCH):
+                fetch_mate(t, c)
+        for step in range(NCH + 3):
+            for lag, stage in enumerate((stage_a, stage_b, stage_c, stage_d)):
+                if 0 <= step - lag < NCH:
+                    stage(step - lag)
+        for q in range(4):
+            eng = nc.scalar if q % 2 else nc.sync
+            eng.dma_start(out=out_2[0, 4 * q : 4 * q + 4, :].bitcast(I32), in_=o_s[32 * q : 32 * q + 4, :].bitcast(I32))

@@ -22,7 +22,7 @@ R = 4
 CH = 128
 NCH = S // CH
 PIECES = [slice(0, 256), slice(256, 384), slice(384, 512)]
-HALVES = [slice(0, 256), slice(256, 512)]
+QUARTERS = [slice(q * 128, (q + 1) * 128) for q in range(4)]
 WHOLE = [slice(0, 512)]
 
 
@@ -47,7 +47,7 @@ def tile_picked_crossfft_none_po_kernel(
         mate_t = tile("mate_t", [P, S // 16], U16)
         xs = tile("xs", [P, T], U8)
         xw = tile("xw", [P, T], I32)
-        w1_raw = [tile(f"w1_raw{u}", [P, R, H // 2], F32) for u in range(2)]
+        w1_raw = [tile(f"w1_raw{u}", [P, 2, H], F32) for u in range(2)]
 
         nc.vector.memset(xs[:].bitcast(I32), 0)
         nc.sync.dma_start(offs_t[:], offs)
@@ -59,8 +59,11 @@ def tile_picked_crossfft_none_po_kernel(
         load_scale_rows(nc.sync, xs, x_scales)
         w1_rows = w1.rearrange("(p j) c -> p j c", j=R)
         for u in range(2):
-            nc.sync.dma_start(out=w1_raw[u][:], in_=w1_rows[:, :, u * (H // 2) : (u + 1) * (H // 2)])
+            nc.sync.dma_start(out=w1_raw[u][:], in_=w1_rows[:, 2 * u : 2 * u + 2, :])
         nc.sync.dma_start(mate_t[:], mate)
+        w3s = tile("w3s", [P, N], U8)
+        nc.gpsimd.memset(w3s[:].bitcast(I32), 0)
+        load_scale_rows(nc.sync, w3s, w3_scales)
         w3w_d = tile("w3w_d", [P, 2 * N], U8)
         nc.vector.tensor_copy(w3w_d[:].rearrange("p (t m e) -> p m t e", t=R, e=2), w3w[:].rearrange("p (m t e) -> p m t e", t=R, e=2))
 
@@ -71,14 +74,14 @@ def tile_picked_crossfft_none_po_kernel(
 
         w1_b = tile("w1_b", [P, R * H], BF16)
         w1_v = w1_b[:].rearrange("p (t m j) -> p m t j", t=R, j=R)
-        nc.scalar.activation(w1_v[:, 0:64], w1_raw[0][:].rearrange("p j (m t) -> p m t j", t=R), COPY)
+        nc.scalar.activation(w1_v[:, :, :, 0:2], w1_raw[0][:].rearrange("p j (m t) -> p m t j", t=R), COPY)
         w1_c = tile("w1_c", [P, H], U32)
         w1_s = tile("w1_s", [P, H], U8)
         w1_hi = w1_raw[1][:].rearrange("p j (m t) -> p m t j", t=R)
         y = [tile(f"y{t}", [P, S], F32) for t in range(R)]
-        nc.scalar.copy(w1_v[:, 64:128, 2:4, :], w1_hi[:, :, 2:4, :])
+        nc.scalar.copy(w1_v[:, :, 2:4, 2:4], w1_hi[:, :, 2:4, :])
         for t in range(2):
-            nc.vector.tensor_copy(w1_v[:, 64:128, t, :], w1_hi[:, :, t, :])
+            nc.vector.tensor_copy(w1_v[:, :, t, 2:4], w1_hi[:, :, t, :])
             cols = slice(t * P, (t + 1) * P)
             nc.vector.quantize_mx(out=w1_c[:, cols].bitcast(FP8X4), scales=w1_s[:, cols], in_=w1_b[:, t * 512 : (t + 1) * 512])
         nc.vector.quantize_mx(out=w1_c[:, 256:512].bitcast(FP8X4), scales=w1_s[:, 256:512], in_=w1_b[:, 1024:2048])
@@ -92,73 +95,87 @@ def tile_picked_crossfft_none_po_kernel(
 
         for t in range(R):
             cols = slice(t * P, (t + 1) * P)
-            product(f"acc_y{t}", ["b0", "a0"] if t == 0 else [f"a{t}"], HALVES if t == 0 else WHOLE, w1_c[:, cols], w1_s[:, cols], xg_w, xg_s,
+            product(f"acc_y{t}", ["b0", "b1", "a0"] if t == 0 else [f"a{t}"], PIECES if t == 0 else WHOLE, w1_c[:, cols], w1_s[:, cols], xg_w, xg_s,
                     lambda acc, cs: nc.scalar.copy(y[t][:, cs], acc[:]))
 
-        w2_raw = [tile(f"w2_raw{u}", [P, R, H // 2], F32, slot=f"w1_raw{u}") for u in range(2)]
-        w2_rows = w2.rearrange("(p j) c -> p j c", j=R)
-        for u in range(2):
-            nc.sync.dma_start(out=w2_raw[u][:], in_=w2_rows[:, :, u * (H // 2) : (u + 1) * (H // 2)])
-        w3s = tile("w3s", [P, N], U8, slot="w1_b")
-        nc.vector.memset(w3s[:].bitcast(I32), 0)
-        load_scale_rows(nc.sync, w3s, w3_scales)
-        res_t = tile("res_t", [P, R, S], F32, slot="xw")
+        w2_raw = tile("w2_raw", [P, R, H], F32, slot="xw")
+        nc.sync.dma_start(out=w2_raw[:], in_=w2.rearrange("(p j) c -> p j c", j=R))
+        w3s_d = tile("w3s_d", [P, N], U8, slot="w1_b")
+        nc.vector.tensor_copy(w3s_d[:].rearrange("p (t m) -> p m t", t=R), w3s[:].rearrange("p (m t) -> p m t", t=R))
+        res_t = tile("res_t", [P, R, S], F32, slot="w1_raw1")
         nc.sync.dma_start(out=res_t[:], in_=res.rearrange("(p t) c -> p t c", t=R))
 
         a = [tile(f"a{t}", [P, V], F32) for t in range(R)]
-        b = [tile(f"b{t}", [P, V], F32) for t in range(R)]
-        nb = [tile(f"nb{t}", [P, V], F32) for t in range(R)]
-        z = [tile(f"z{t}", [P, S], F32) for t in range(R)]
-        z_b = tile("z_b", [P, S, R], BF16)
+        b = tile("b", [P, R, V], F32)
+        nb_first = tile("nb_first", [P, R - 1, V], F32, slot="w1_c")
+        z = [tile(f"z{t}", [P, S], F32) for t in range(R - 1)]
         w2_b = tile("w2_b", [P, R * H], BF16)
         w2_v = w2_b[:].rearrange("p (t m j) -> p m t j", t=R, j=R)
-        w2_in = [w2_raw[u][:].rearrange("p j (m t) -> p m t j", t=R) for u in range(2)]
-
-        def fetch_b(t):
-            nc.vector.tensor_copy(b[t][:], y[t][:].indirect(lb_t[:]))
-            nc.scalar.activation(nb[t][:], b[t][:], COPY, scale=-1.0)
-
-        def fetch_a(t):
-            nc.vector.tensor_copy(a[t][:], y[t][:].indirect(la_t[:]))
-
-        fetch_b(0)
-        fetch_a(0)
+        w2_in = w2_raw[:].rearrange("p j (m t) -> p m t j", t=R)
         for t in range(R):
-            if t + 1 < R:
-                fetch_b(t + 1)
-            nc.vector.tensor_tensor(z[t][:].indirect(la_t[:]), a[t][:], b[t][:], ADD)
-            if t + 1 < R:
-                fetch_a(t + 1)
-            nc.vector.tensor_tensor(z[t][:].indirect(lb_t[:]), a[t][:], nb[t][:], ADD)
-            nc.scalar.copy(w2_v[:, 32 * t : 32 * t + 32], w2_in[t // 2][:, 32 * (t % 2) : 32 * (t % 2) + 32])
-            for cols in PIECES:
-                nc.scalar.copy(z_b[:, cols, t], z[t][:, cols])
+            nc.vector.tensor_copy(b[:, t, :], y[t][:].indirect(lb_t[:]))
+            nc.vector.tensor_copy(a[t][:], y[t][:].indirect(la_t[:]))
+        nc.scalar.activation(nb_first[:], b[:, 0 : R - 1, :], COPY, scale=-1.0)
+        nc.scalar.copy(w2_v, w2_in)
+        z_b = tile("z_b", [P, S, R], BF16, slot="xw")
 
-        w2_c = tile("w2_c", [P, H], U32, slot="a3")
+        def put_difference(t, nb):
+            nc.vector.tensor_tensor(z[t][:].indirect(lb_t[:]), a[t][:], nb, ADD)
+
+        def put_sum(t):
+            nc.vector.tensor_tensor(z[t][:].indirect(la_t[:]), a[t][:], b[:, t, :], ADD)
+
+        def weave(t):
+            nc.scalar.copy(z_b[:, :, t], z[t][:])
+
+        put_difference(2, nb_first[:, 2, :])
+        put_difference(0, nb_first[:, 0, :])
+        put_sum(2)
+        weave(2)
+        put_difference(1, nb_first[:, 1, :])
+        put_sum(0)
+        weave(0)
+        put_sum(1)
+        weave(1)
+        z.append(tile("z3", [P, S], F32, slot="a0"))
+        put_sum(3)
+        w2_c0 = tile("w2_c0", [P, P], U32, slot="a1")
         w2_s = tile("w2_s", [P, H], U8)
-        nc.vector.quantize_mx(out=w2_c[:].bitcast(FP8X4), scales=w2_s[:], in_=w2_b[:])
+        nc.vector.quantize_mx(out=w2_c0[:].bitcast(FP8X4), scales=w2_s[:, 0:P], in_=w2_b[:, 0:512])
+        nb_last = tile("nb_last", [P, V], F32, slot="z2")
+        nc.scalar.activation(nb_last[:], b[:, R - 1, :], COPY, scale=-1.0)
+        put_difference(3, nb_last[:])
+        for cols in QUARTERS[:2]:
+            nc.scalar.copy(z_b[:, cols, 3], z[3][:, cols])
+        for cols in QUARTERS[2:]:
+            nc.vector.tensor_copy(z_b[:, cols, 3], z[3][:, cols])
 
         z_c = tile("z_c", [P, S], U32)
         z_s = tile("z_s", [P, S], U8)
-        for cols in PIECES:
+        z_order = [QUARTERS[q] for q in (0, 2, 3, 1)]
+        for cols in z_order:
             nc.vector.quantize_mx(out=z_c[:, cols].bitcast(FP8X4), scales=z_s[:, cols],
                                   in_=z_b[:, cols, :].rearrange("p c t -> p (c t)"))
 
-        w3s_d = tile("w3s_d", [P, N], U8, slot="z_b")
-        nc.vector.tensor_copy(w3s_d[:].rearrange("p (t m) -> p m t", t=R), w3s[:].rearrange("p (m t) -> p m t", t=R))
+        w2_c = tile("w2_c", [P, H - P], U32, slot="xw")
+        nc.vector.quantize_mx(out=w2_c[:, 0:P].bitcast(FP8X4), scales=w2_s[:, P : 2 * P], in_=w2_b[:, 512:1024])
+        nc.vector.quantize_mx(out=w2_c[:, P:].bitcast(FP8X4), scales=w2_s[:, 2 * P :], in_=w2_b[:, 1024:2048])
         hneg = [tile(f"hneg{t}", [P, S], F32) for t in range(R)]
+        late = {}
         hpos = [tile(f"hpos{t}", [P, S], F32) for t in range(R)]
         for t in range(R):
             wc = slice(t * P, (t + 1) * P)
 
             def leave(acc, cs):
                 nc.scalar.activation(hneg[t][:, cs], acc[:], COPY, scale=-1.0)
-                if t == 0:
+                if t == 0 and cs is not z_order[-1]:
                     nc.vector.tensor_scalar(hpos[t][:, cs], hneg[t][:, cs], -1.0, None, MULT)
-                else:
+                elif t < 2:
                     nc.scalar.copy(hpos[t][:, cs], acc[:])
+                else:
+                    late[t] = acc
 
-            product(f"acc_h{t}", ["b0", "a0", "a1"] if t == 0 else [f"b{t}"], PIECES if t == 0 else WHOLE, w2_c[:, wc], w2_s[:, wc], z_c, z_s, leave)
+            product(f"acc_h{t}", ["b0", "a0", "a1", "a2"] if t == 0 else [f"b{t}"], z_order if t == 0 else WHOLE, w2_c0[:] if t == 0 else w2_c[:, (t - 1) * P : t * P], w2_s[:, wc], z_c, z_s, leave)
 
         z2 = [tile(f"z2_{c}", [P, R, CH], F32) for c in range(NCH)]
 
@@ -183,10 +200,13 @@ def tile_picked_crossfft_none_po_kernel(
             else:
                 nc.scalar.copy(dst[:], src[:].rearrange("p t c -> p c t"))
 
-        def stage_a(c):
+        def stage_0(c):
             for t in range(2, R):
+                nc.scalar.copy(hpos[t][:, c * CH : (c + 1) * CH], late[t][:, c * CH : (c + 1) * CH])
                 fetch_mate(t, c)
-            interleave(c, z2_b[c], z2[c])
+
+        def stage_a(c):
+            nc.scalar.copy(z2_b[c][:], z2[c][:].rearrange("p t c -> p c t"))
 
         def stage_b(c):
             nc.vector.quantize_mx(out=z2_c[c][:].bitcast(FP8X4), scales=z2_s[c][:], in_=z2_b[c][:].rearrange("p c t -> p (c t)"))
@@ -206,11 +226,12 @@ def tile_picked_crossfft_none_po_kernel(
             nc.vector.quantize_mx(out=o_w[:, cols].bitcast(FP8X4), scales=o_s[:, cols], in_=o_b[c][:].rearrange("p c t -> p (c t)"))
             nc.sync.dma_start(out=words[:, cols], in_=o_w[:, cols].bitcast(I32))
 
-        for t in range(2):
-            for c in range(NCH):
-                fetch_mate(t, c)
-        for step in range(NCH + 3):
-            for lag, stage in enumerate((stage_a, stage_b, stage_c, stage_d)):
+        for c in (0, 2, 3, 1):
+            fetch_mate(0, c)
+        for c in range(NCH):
+            fetch_mate(1, c)
+        for step in range(NCH + 4):
+            for lag, stage in enumerate((stage_0, stage_a, stage_b, stage_c, stage_d)):
                 if 0 <= step - lag < NCH:
                     stage(step - lag)
         for q in range(4):

from contextlib import ExitStack

import concourse.mybir as mybir

K, T, S, V, N, H = 512, 2048, 512, 256, 512, 512
FLOPS = 2 * K * H * S + 2 * H * H * S + 2 * H * N * S

F32 = mybir.dt.float32
BF16 = mybir.dt.bfloat16
I32 = mybir.dt.int32
U32 = mybir.dt.uint32
U16 = mybir.dt.uint16
U8 = mybir.dt.uint8
FP8X4 = mybir.dt.float8_e4m3fn_x4
FP4X4 = mybir.dt.float4_e2m1fn_x4
ADD = mybir.AluOpType.add
MULT = mybir.AluOpType.mult
COPY = mybir.ActivationFunctionType.Copy

P = 128
R = 4
CH = 128
NCH = S // CH
PIECES = [slice(0, 256), slice(256, 384), slice(384, 512)]
QUARTERS = [slice(q * 128, (q + 1) * 128) for q in range(4)]
WHOLE = [slice(0, 512)]


def tile_picked_crossfft_none_po_kernel(
    tc, x_words, x_scales, w1, w2, res, w3_words, w3_scales, offs, la, lb, mate, out_0, out_1, out_2
):
    nc = tc.nc
    with ExitStack() as ctx:
        sb = ctx.enter_context(tc.tile_pool(name="sb", bufs=1))
        ps = ctx.enter_context(tc.psum_pool(name="ps", bufs=1))

        def tile(name, shape, dtype, slot=None):
            return sb.tile(shape, dtype, name=name, tag=slot or name, align_bytes=64)

        def load_scale_rows(eng, dst, src):
            for q in range(4):
                eng.dma_start(out=dst[32 * q : 32 * q + 4, :].bitcast(I32), in_=src[0, 4 * q : 4 * q + 4, :].bitcast(I32))

        offs_t = tile("offs_t", [P, S // 16], U16)
        la_t = tile("la_t", [P, V // 16], U16)
        lb_t = tile("lb_t", [P, V // 16], U16)
        mate_t = tile("mate_t", [P, S // 16], U16)
        xs = tile("xs", [P, T], U8)
        xw = tile("xw", [P, T], I32)
        w1_raw = [tile(f"w1_raw{u}", [P, 2, H], F32) for u in range(2)]

        nc.vector.memset(xs[:].bitcast(I32), 0)
        nc.sync.dma_start(offs_t[:], offs)
        w3w = tile("w3w", [P, 2 * N], U8)
        nc.sync.dma_start(out=w3w[:].bitcast(I32), in_=w3_words[0].bitcast(I32))
        nc.sync.dma_start(la_t[:], la)
        nc.sync.dma_start(out=xw[:], in_=x_words[0].rearrange("p n r -> p (n r)").bitcast(I32))
        nc.sync.dma_start(lb_t[:], lb)
        load_scale_rows(nc.sync, xs, x_scales)
        w1_rows = w1.rearrange("(p j) c -> p j c", j=R)
        for u in range(2):
            nc.sync.dma_start(out=w1_raw[u][:], in_=w1_rows[:, 2 * u : 2 * u + 2, :])
        nc.sync.dma_start(mate_t[:], mate)
        w3s = tile("w3s", [P, N], U8)
        nc.gpsimd.memset(w3s[:].bitcast(I32), 0)
        load_scale_rows(nc.sync, w3s, w3_scales)
        w3w_d = tile("w3w_d", [P, 2 * N], U8)
        nc.vector.tensor_copy(w3w_d[:].rearrange("p (t m e) -> p m t e", t=R, e=2), w3w[:].rearrange("p (m t e) -> p m t e", t=R, e=2))

        xg_s = tile("xg_s", [P, S], U8)
        xg_w = tile("xg_w", [P, S], U32)
        nc.vector.tensor_copy(xg_w[:], xw[:].bitcast(U32).indirect(offs_t[:]))
        nc.vector.tensor_copy(xg_s[:], xs[:].indirect(offs_t[:]))

        w1_b = tile("w1_b", [P, R * H], BF16)
        w1_v = w1_b[:].rearrange("p (t m j) -> p m t j", t=R, j=R)
        nc.scalar.activation(w1_v[:, :, :, 0:2], w1_raw[0][:].rearrange("p j (m t) -> p m t j", t=R), COPY)
        w1_c = tile("w1_c", [P, H], U32)
        w1_s = tile("w1_s", [P, H], U8)
        w1_hi = w1_raw[1][:].rearrange("p j (m t) -> p m t j", t=R)
        y = [tile(f"y{t}", [P, S], F32) for t in range(R)]
        nc.scalar.copy(w1_v[:, :, 2:4, 2:4], w1_hi[:, :, 2:4, :])
        for t in range(2):
            nc.vector.tensor_copy(w1_v[:, :, t, 2:4], w1_hi[:, :, t, :])
            cols = slice(t * P, (t + 1) * P)
            nc.vector.quantize_mx(out=w1_c[:, cols].bitcast(FP8X4), scales=w1_s[:, cols], in_=w1_b[:, t * 512 : (t + 1) * 512])
        nc.vector.quantize_mx(out=w1_c[:, 256:512].bitcast(FP8X4), scales=w1_s[:, 256:512], in_=w1_b[:, 1024:2048])

        def product(name, tags, pieces, codes, scales, rhs, rhs_scale, leave):
            for tag, cols in zip(tags, pieces):
                acc = ps.tile([P, cols.stop - cols.start], F32, name=f"{name}_{tag}", tag=tag)
                nc.tensor.matmul_mx(out=acc[:], lhsT=codes.bitcast(FP8X4), lhsT_scale=scales,
                                    rhs=rhs[:, cols].bitcast(FP8X4), rhs_scale=rhs_scale[:, cols], start=True, stop=True)
                leave(acc, cols)

        for t in range(R):
            cols = slice(t * P, (t + 1) * P)
            product(f"acc_y{t}", ["b0", "b1", "a0"] if t == 0 else [f"a{t}"], PIECES if t == 0 else WHOLE, w1_c[:, cols], w1_s[:, cols], xg_w, xg_s,
                    lambda acc, cs: nc.scalar.copy(y[t][:, cs], acc[:]))

        w2_raw = tile("w2_raw", [P, R, H], F32, slot="xw")
        nc.sync.dma_start(out=w2_raw[:], in_=w2.rearrange("(p j) c -> p j c", j=R))
        w3s_d = tile("w3s_d", [P, N], U8, slot="w1_b")
        nc.vector.tensor_copy(w3s_d[:].rearrange("p (t m) -> p m t", t=R), w3s[:].rearrange("p (m t) -> p m t", t=R))
        res_t = tile("res_t", [P, R, S], F32, slot="w1_raw1")
        nc.sync.dma_start(out=res_t[:], in_=res.rearrange("(p t) c -> p t c", t=R))

        a = [tile(f"a{t}", [P, V], F32) for t in range(R)]
        b = tile("b", [P, R, V], F32)
        nb_first = tile("nb_first", [P, R - 1, V], F32, slot="w1_c")
        z = [tile(f"z{t}", [P, S], F32) for t in range(R - 1)]
        w2_b = tile("w2_b", [P, R * H], BF16)
        w2_v = w2_b[:].rearrange("p (t m j) -> p m t j", t=R, j=R)
        w2_in = w2_raw[:].rearrange("p j (m t) -> p m t j", t=R)
        for t in range(R):
            nc.vector.tensor_copy(b[:, t, :], y[t][:].indirect(lb_t[:]))
            nc.vector.tensor_copy(a[t][:], y[t][:].indirect(la_t[:]))
        nc.scalar.activation(nb_first[:], b[:, 0 : R - 1, :], COPY, scale=-1.0)
        nc.scalar.copy(w2_v, w2_in)
        z_b = tile("z_b", [P, S, R], BF16, slot="xw")

        def put_difference(t, nb):
            nc.vector.tensor_tensor(z[t][:].indirect(lb_t[:]), a[t][:], nb, ADD)

        def put_sum(t):
            nc.vector.tensor_tensor(z[t][:].indirect(la_t[:]), a[t][:], b[:, t, :], ADD)

        def weave(t):
            nc.scalar.copy(z_b[:, :, t], z[t][:])

        put_difference(2, nb_first[:, 2, :])
        put_difference(0, nb_first[:, 0, :])
        put_sum(2)
        weave(2)
        put_difference(1, nb_first[:, 1, :])
        put_sum(0)
        weave(0)
        put_sum(1)
        weave(1)
        z.append(tile("z3", [P, S], F32, slot="a0"))
        put_sum(3)
        w2_c0 = tile("w2_c0", [P, P], U32, slot="a1")
        w2_s = tile("w2_s", [P, H], U8)
        nc.vector.quantize_mx(out=w2_c0[:].bitcast(FP8X4), scales=w2_s[:, 0:P], in_=w2_b[:, 0:512])
        nb_last = tile("nb_last", [P, V], F32, slot="z2")
        nc.scalar.activation(nb_last[:], b[:, R - 1, :], COPY, scale=-1.0)
        put_difference(3, nb_last[:])
        for cols in QUARTERS[:2]:
            nc.scalar.copy(z_b[:, cols, 3], z[3][:, cols])
        for cols in QUARTERS[2:]:
            nc.vector.tensor_copy(z_b[:, cols, 3], z[3][:, cols])

        z_c = tile("z_c", [P, S], U32)
        z_s = tile("z_s", [P, S], U8)
        z_order = [QUARTERS[q] for q in (0, 2, 3, 1)]
        for cols in z_order:
            nc.vector.quantize_mx(out=z_c[:, cols].bitcast(FP8X4), scales=z_s[:, cols],
                                  in_=z_b[:, cols, :].rearrange("p c t -> p (c t)"))

        w2_c = tile("w2_c", [P, H - P], U32, slot="xw")
        nc.vector.quantize_mx(out=w2_c[:, 0:P].bitcast(FP8X4), scales=w2_s[:, P : 2 * P], in_=w2_b[:, 512:1024])
        nc.vector.quantize_mx(out=w2_c[:, P:].bitcast(FP8X4), scales=w2_s[:, 2 * P :], in_=w2_b[:, 1024:2048])
        hneg = [tile(f"hneg{t}", [P, S], F32) for t in range(R)]
        late = {}
        hpos = [tile(f"hpos{t}", [P, S], F32) for t in range(R)]
        for t in range(R):
            wc = slice(t * P, (t + 1) * P)

            def leave(acc, cs):
                nc.scalar.activation(hneg[t][:, cs], acc[:], COPY, scale=-1.0)
                if t == 0 and cs is not z_order[-1]:
                    nc.vector.tensor_scalar(hpos[t][:, cs], hneg[t][:, cs], -1.0, None, MULT)
                elif t < 2:
                    nc.scalar.copy(hpos[t][:, cs], acc[:])
                else:
                    late[t] = acc

            product(f"acc_h{t}", ["b0", "a0", "a1", "a2"] if t == 0 else [f"b{t}"], z_order if t == 0 else WHOLE, w2_c0[:] if t == 0 else w2_c[:, (t - 1) * P : t * P], w2_s[:, wc], z_c, z_s, leave)

        z2 = [tile(f"z2_{c}", [P, R, CH], F32) for c in range(NCH)]

        def fetch_mate(t, c):
            nc.vector.tensor_tensor(z2[c][:, t, :], hneg[t][:].indirect(mate_t[:, c * CH // 16 : (c + 1) * CH // 16]),
                                    hpos[t][:, c * CH : (c + 1) * CH], ADD)

        o_w = tile("o_w", [P, S], U32)
        o_s = tile("o_s", [P, S], U8)
        out_rows = out_0.rearrange("(p t) c -> p t c", t=R)
        words = out_1[0].rearrange("p c r -> p (c r)").bitcast(I32)
        z2_b = [tile(f"z2_b{c}", [P, CH, R], BF16) for c in range(NCH)]
        z2_c = [tile(f"z2_c{c}", [P, CH], U32) for c in range(NCH)]
        z2_s = [tile(f"z2_s{c}", [P, CH], U8) for c in range(NCH)]
        o = [tile(f"o{c}", [P, R, CH], F32) for c in range(NCH)]
        o_b = [tile(f"o_b{c}", [P, CH, R], BF16) for c in range(NCH)]
        accs = {}

        def interleave(c, dst, src):
            if c == NCH - 1:
                nc.vector.tensor_copy(dst[:], src[:].rearrange("p t c -> p c t"))
            else:
                nc.scalar.copy(dst[:], src[:].rearrange("p t c -> p c t"))

        def stage_0(c):
            for t in range(2, R):
                nc.scalar.copy(hpos[t][:, c * CH : (c + 1) * CH], late[t][:, c * CH : (c + 1) * CH])
                fetch_mate(t, c)

        def stage_a(c):
            nc.scalar.copy(z2_b[c][:], z2[c][:].rearrange("p t c -> p c t"))

        def stage_b(c):
            nc.vector.quantize_mx(out=z2_c[c][:].bitcast(FP8X4), scales=z2_s[c][:], in_=z2_b[c][:].rearrange("p c t -> p (c t)"))
            accs[c] = ps.tile([P, R, CH], F32, name=f"acc_o{c}", tag=f"a{c}")
            for t in range(R):
                nc.tensor.matmul_mx(out=accs[c][:, t, :], lhsT=w3w_d[:, 2 * t * P : 2 * (t + 1) * P].bitcast(FP4X4),
                                    lhsT_scale=w3s_d[:, t * P : (t + 1) * P],
                                    rhs=z2_c[c][:].bitcast(FP8X4), rhs_scale=z2_s[c][:], start=True, stop=True)

        def stage_c(c):
            nc.vector.scalar_tensor_tensor(o[c][:], accs[c][:], 0.5, res_t[:, :, c * CH : (c + 1) * CH], MULT, ADD)
            nc.sync.dma_start(out=out_rows[:, :, c * CH : (c + 1) * CH], in_=o[c][:])
            interleave(c, o_b[c], o[c])

        def stage_d(c):
            cols = slice(c * CH, (c + 1) * CH)
            nc.vector.quantize_mx(out=o_w[:, cols].bitcast(FP8X4), scales=o_s[:, cols], in_=o_b[c][:].rearrange("p c t -> p (c t)"))
            nc.sync.dma_start(out=words[:, cols], in_=o_w[:, cols].bitcast(I32))

        for c in (0, 2, 3, 1):
            fetch_mate(0, c)
        for c in range(NCH):
            fetch_mate(1, c)
        for step in range(NCH + 4):
            for lag, stage in enumerate((stage_0, stage_a, stage_b, stage_c, stage_d)):
                if 0 <= step - lag < NCH:
                    stage(step - lag)
        for q in range(4):
            eng = nc.scalar if q % 2 else nc.sync
            eng.dma_start(out=out_2[0, 4 * q : 4 * q + 4, :].bitcast(I32), in_=o_s[32 * q : 32 * q + 4, :].bitcast(I32))
